import numpy as np
import ml_dtypes


def mxq(x, axis, fmt="e4m3"):
    dtype, down = {"e4m3": (ml_dtypes.float8_e4m3fn, 7), "e5m2": (ml_dtypes.float8_e5m2, 14)}[fmt]
    v = np.moveaxis(np.asarray(x, np.float32).astype(ml_dtypes.bfloat16).astype(np.float64), axis, -1)
    blocks = v.reshape(v.shape[:-1] + (-1, 32))
    amax = np.abs(blocks).max(-1, keepdims=True)
    byte = np.maximum(np.where(amax > 0, np.frexp(amax)[1] - 1 + 127, 0) - down, 1)
    scale = np.exp2(byte - 127.0)
    codes = (blocks / scale).astype(np.float32).astype(dtype).astype(np.float64)
    return np.moveaxis((codes * scale).reshape(v.shape), -1, axis)


WIDE = False


def mx_kscale(k):
    if not WIDE:
        return np.ones(k)
    levels = np.array([30, -30])
    if k % 512:
        return np.exp2(np.random.permutation(np.resize(levels, k // 32))).repeat(32)
    a = np.empty((k // 512, 16))
    for p in range(k // 512):
        a[p, :8] = np.random.permutation(np.resize(levels, 8))
        for g in range(8):
            far = levels[np.abs(levels - a[p, g]) >= 10]
            a[p, g + 8] = far[np.random.randint(len(far))]
    return np.exp2(a.ravel()).repeat(32)


def f64(x):
    return np.asarray(x).astype(np.float64)


def striped(idx):
    return np.tile(np.asarray(idx).reshape(-1, 16).T, (8, 1)).astype(np.uint16)


def unstriped(offs):
    return offs[:16].T.reshape(-1).astype(np.int64)


E2M1 = np.array([0.0, 0.5, 1.0, 1.5, 2.0, 3.0, 4.0, 6.0, -0.0, -0.5, -1.0, -1.5, -2.0, -3.0, -4.0, -6.0])


def pack_weight(w, fmt):
    k, n = w.shape
    w = f64(np.asarray(w, np.float32).astype(ml_dtypes.bfloat16)).reshape(k // 32, 32, n)
    amax = np.abs(w).max(1)
    if fmt in ("e4m3", "e5m2"):
        byte = np.frexp(amax)[1] - 1 + 127 - (7 if fmt == "e4m3" else 14)
    else:
        mant, ex = np.frexp(amax / 6.0)
        byte = np.where(mant > 0.5, ex, ex - 1) + 127
    byte = np.clip(np.where(amax > 0, byte, 1), 1, 254)
    scaled = (w * np.exp2(127.0 - byte)[:, None, :]).reshape(k, n).astype(np.float32)
    by_word = np.ascontiguousarray(scaled.reshape(k // 512, 128, 4, n).transpose(0, 1, 3, 2))
    if fmt in ("e4m3", "e5m2"):
        words = by_word.astype(ml_dtypes.float8_e4m3fn if fmt == "e4m3" else ml_dtypes.float8_e5m2).view(np.uint8)
    else:
        c = by_word.astype(ml_dtypes.float4_e2m1fn).view(np.uint8) & 0xF
        words = (c[..., 0::2] | (c[..., 1::2] << 4)).reshape(k // 512, 128, 2 * n)
    return np.ascontiguousarray(words), np.ascontiguousarray(byte.astype(np.uint8).reshape(k // 512, 16, n))


def unpack_weight(words, scales, fmt):
    g, _, n = scales.shape
    words = np.ascontiguousarray(words).reshape(g, 128, n, -1)
    if fmt in ("e4m3", "e5m2"):
        vals = words.view(ml_dtypes.float8_e4m3fn if fmt == "e4m3" else ml_dtypes.float8_e5m2).astype(np.float64)
    else:
        nib = np.empty((g, 128, n, 4), np.uint8)
        nib[..., 0::2] = words & 0xF
        nib[..., 1::2] = words >> 4
        vals = E2M1[nib]
    vals = vals * np.repeat(np.exp2(scales.astype(np.float64) - 127.0), 8, axis=1)[..., None]
    return vals.transpose(0, 1, 3, 2).reshape(g * 512, n)


K, T, J, R, F, Z, C, O, N, L = 512, 1024, 256, 512, 512, 1024, 512, 128, 256, 512


def setup_inputs():
    n = np.random.standard_normal
    idx = np.random.permutation(T)[:J]
    idx2 = np.random.permutation(Z)[:J]
    idx3 = np.random.permutation(C)[:J]
    idx4 = np.random.permutation(C)[:J]
    idx5 = np.random.permutation(J)[:J]
    idx6 = np.random.permutation(J)[:O]
    idx7 = np.random.permutation(J)[:O]
    ff = mx_kscale(F)
    fk = mx_kscale(K)
    fr = mx_kscale(R)
    fl = mx_kscale(L)
    xop = pack_weight(n((F, Z)) / ff[:, None], "e2m1")
    wp = pack_weight(n((K, R)) * 1 / np.sqrt(K) / fk[:, None] * fr, "e2m1")
    w2p = pack_weight(n((F, R)) * 1 / np.sqrt(F) * ff[:, None], "e5m2")
    wbp = pack_weight(n((R, N)) * 1 / np.sqrt(R) / fr[:, None], "e5m2")
    sxp = pack_weight(n((L, O)) / fl[:, None], "e2m1")
    wsp = pack_weight(n((L, N)) * 1 / np.sqrt(L) * fl[:, None], "e5m2")
    return {
        "xo_words": xop[0],
        "xo_scales": xop[1],
        "cq": (np.random.randint(-7, 8, (K, T)).astype(np.float64)).astype(np.float32),
        "gs": (np.random.uniform(0.1, 0.4, (K, 1)) * fk[:, None]).astype(np.float32),
        "w_words": wp[0],
        "w_scales": wp[1],
        "w2_words": w2p[0],
        "w2_scales": w2p[1],
        "wb_words": wbp[0],
        "wb_scales": wbp[1],
        "sx_words": sxp[0],
        "sx_scales": sxp[1],
        "ws_words": wsp[0],
        "ws_scales": wsp[1],
        "offs": striped(idx),
        "offs2": striped(idx2),
        "offs3": striped(idx3),
        "offs4": striped(idx4),
        "offs5": striped(idx5),
        "offs6": striped(idx6),
        "offs7": striped(idx7),
    }


def reference(xo_words, xo_scales, cq, gs, w_words, w_scales, w2_words, w2_scales, wb_words, wb_scales, sx_words, sx_scales, ws_words, ws_scales, offs, offs2, offs3, offs4, offs5, offs6, offs7):
    idx = unstriped(offs)
    idx2 = unstriped(offs2)
    idx3 = unstriped(offs3)
    idx4 = unstriped(offs4)
    idx5 = unstriped(offs5)
    idx6 = unstriped(offs6)
    idx7 = unstriped(offs7)
    xou = unpack_weight(xo_words, xo_scales, "e2m1")
    wu = unpack_weight(w_words, w_scales, "e2m1")
    w2u = unpack_weight(w2_words, w2_scales, "e5m2")
    wbu = unpack_weight(wb_words, wb_scales, "e5m2")
    sxu = unpack_weight(sx_words, sx_scales, "e2m1")
    wsu = unpack_weight(ws_words, ws_scales, "e5m2")
    x1 = f64(cq)[:, idx] * f64(gs)
    x1q = mxq(x1, 0, "e4m3")
    a = wu.T @ x1q
    xoidx2g = xou[:, idx2]
    b = w2u.T @ xoidx2g
    lb = b[:, 0:1]
    la = a[:, 0:1]
    lb2 = b[:, 128:129]
    pw = np.zeros((R, C))
    pw[:, idx3] = a
    rb = np.maximum(pw[:, idx4] * lb, b[:, idx5] * la)
    hid = np.abs(rb[:, idx6] - rb[:, idx7] * lb2)
    hidq = mxq(hid, 0, "e4m3")
    y = wbu.T @ hidq + wsu.T @ sxu
    return y

@@ -1,0 +1,177 @@
+from contextlib import ExitStack
+
+import concourse.mybir as mybir
+
+K, T, J, R, F, Z, C, O, N, L = 512, 1024, 256, 512, 512, 1024, 512, 128, 256, 512
+FLOPS = 2 * K * R * J + 2 * F * R * J + 2 * R * N * O + 2 * L * N * O
+
+F32 = mybir.dt.float32
+BF16 = mybir.dt.bfloat16
+I32 = mybir.dt.int32
+U32 = mybir.dt.uint32
+U16 = mybir.dt.uint16
+U8 = mybir.dt.uint8
+E4M3 = mybir.dt.float8_e4m3fn_x4
+E5M2 = mybir.dt.float8_e5m2_x4
+E2M1 = mybir.dt.float4_e2m1fn_x4
+COPY = mybir.ActivationFunctionType.Copy
+ABS = mybir.ActivationFunctionType.Abs
+ALU = mybir.AluOpType
+
+P = 128
+PACK = 4
+QUADS = 4
+
+
+def tile_list_leadanswer_codednote_further_plain_kernel(
+    tc, xo_words, xo_scales, cq, gs, w_words, w_scales, w2_words, w2_scales, wb_words, wb_scales,
+    sx_words, sx_scales, ws_words, ws_scales, offs, offs2, offs3, offs4, offs5, offs6, offs7, out,
+):
+    nc = tc.nc
+    with ExitStack() as ctx:
+        lists = ctx.enter_context(tc.tile_pool(name="lists", bufs=1))
+        sb = ctx.enter_context(tc.tile_pool(name="sb", bufs=1))
+        psum = ctx.enter_context(tc.psum_pool(name="psum", bufs=1))
+
+        def load_list(ap, name):
+            t = lists.tile([P, ap.shape[1]], U16, name=name)
+            nc.sync.dma_start(t[:], ap)
+            return t
+
+        def staged_rows(scales):
+            return scales[0].rearrange("(q r) c -> r q c", r=4).bitcast(I32)
+
+        ww_stage = sb.tile([4, QUADS, 2 * R // 4], I32, name="ww_stage")
+        xo_stage = sb.tile([4, QUADS, Z // 4], I32, name="xo_stage")
+        nc.scalar.dma_start(ww_stage[:, :, 0 : R // 4], staged_rows(w_scales))
+        nc.scalar.dma_start(ww_stage[:, :, R // 4 :], staged_rows(w2_scales))
+        nc.scalar.dma_start(xo_stage[:], staged_rows(xo_scales))
+
+        l1 = load_list(offs, "l1")
+        gs_t = sb.tile([P, PACK], F32, name="gs_t")
+        nc.sync.dma_start(gs_t[:], gs.rearrange("(p t) o -> p (t o)", t=PACK))
+        cq_rows = cq.rearrange("(p t) c -> t p c", t=PACK)
+        cq_t = [sb.tile([P, T], F32, name="cq%d" % t) for t in range(PACK)]
+        nc.sync.dma_start(cq_t[0][:], cq_rows[0])
+        nc.sync.dma_start(cq_t[1][:], cq_rows[1])
+        l2 = load_list(offs2, "l2")
+        nc.sync.dma_start(cq_t[2][:], cq_rows[2])
+        nc.sync.dma_start(cq_t[3][:], cq_rows[3])
+        w_raw = sb.tile([P, R], U16, name="w_raw")
+        nc.sync.dma_start(w_raw[:].bitcast(I32), w_words[0].bitcast(I32))
+        xo_raw = sb.tile([P, Z], U16, name="xo_raw")
+        nc.sync.dma_start(xo_raw[:].bitcast(I32), xo_words[0].bitcast(I32))
+        w2_raw = sb.tile([P, R], U32, name="w2_raw")
+        nc.sync.dma_start(w2_raw[:].bitcast(I32), w2_words[0].rearrange("p n t -> p (n t)").bitcast(I32))
+        l3 = load_list(offs3, "l3")
+        l5 = load_list(offs5, "l5")
+        l4 = load_list(offs4, "l4")
+        l7 = load_list(offs7, "l7")
+        l6 = load_list(offs6, "l6")
+        ws_c = sb.tile([P, N], U32, name="ws_c", align_bytes=64)
+        nc.sync.dma_start(ws_c[:].bitcast(I32), ws_words[0].rearrange("p n t -> p (n t)").bitcast(I32))
+        sx_c = sb.tile([P, O], U16, name="sx_c", align_bytes=64)
+        nc.sync.dma_start(sx_c[:].bitcast(I32), sx_words[0].bitcast(I32))
+        wb_c = sb.tile([P, N], U32, name="wb_c", align_bytes=64)
+        nc.sync.dma_start(wb_c[:].bitcast(I32), wb_words[0].rearrange("p n t -> p (n t)").bitcast(I32))
+
+        ww_plane = sb.tile([P, 2 * R], U8, name="ww_plane")
+        xo_plane = sb.tile([P, Z], U8, name="xo_plane")
+        ws_s = sb.tile([P, N], U8, name="ws_s", align_bytes=64)
+        sx_s = sb.tile([P, O], U8, name="sx_s", align_bytes=64)
+        wb_s = sb.tile([P, N], U8, name="wb_s", align_bytes=64)
+        x1_s = sb.tile([P, J], U8, name="x1_s", align_bytes=64)
+        hid_s = sb.tile([P, O], U8, name="hid_s", align_bytes=64)
+        for plane in (ww_plane, xo_plane, ws_s, sx_s, wb_s):
+            nc.vector.memset(plane[:].bitcast(I32), 0)
+        pw = [sb.tile([P, C], F32, name="pw%d" % t) for t in range(PACK)]
+        for t in range(PACK):
+            nc.vector.memset(pw[t][:], 0.0)
+
+        for plane, scales in ((ws_s, ws_scales), (sx_s, sx_scales), (wb_s, wb_scales)):
+            for q in range(QUADS):
+                nc.sync.dma_start(plane[32 * q : 32 * q + 4, :].bitcast(I32), scales[0, 4 * q : 4 * q + 4, :].bitcast(I32))
+
+        x1_planes = sb.tile([P, PACK, J], BF16, name="x1_planes")
+        for t in range(PACK):
+            nc.scalar.activation(x1_planes[:, t, :], cq_t[t][:].indirect(l1[:]), COPY, scale=gs_t[:, t : t + 1])
+        x1_w = sb.tile([P, J, PACK], BF16, name="x1_w", align_bytes=64)
+        nc.vector.tensor_copy(
+            x1_w[:].rearrange("p (c i) t -> p c t i", i=4), x1_planes[:].rearrange("p t (c i) -> p c t i", i=4)
+        )
+        x1_c = sb.tile([P, J], U32, name="x1_c", align_bytes=64)
+        nc.vector.quantize_mx(x1_c[:].bitcast(E4M3), x1_s[:], x1_w[:].rearrange("p j t -> p (j t)"))
+
+        for q in range(QUADS):
+            nc.vector.tensor_copy(ww_plane[32 * q : 32 * q + 4, :].bitcast(I32), ww_stage[:, q, :])
+        ww_s = sb.tile([P, 2, PACK, P], U8, name="ww_s", align_bytes=64)
+        nc.vector.tensor_copy(ww_s[:], ww_plane[:].rearrange("p (u m t) -> p u t m", u=2, t=PACK))
+        for q in range(QUADS):
+            nc.vector.tensor_copy(xo_plane[32 * q : 32 * q + 4, :].bitcast(I32), xo_stage[:, q, :])
+        xo_s = sb.tile([P, J], U8, name="xo_s", align_bytes=64)
+        nc.vector.tensor_copy(xo_s[:], xo_plane[:].indirect(l2[:]))
+
+        w_c = sb.tile([P, PACK, P], U16, name="w_c", align_bytes=64)
+        nc.scalar.copy(w_c[:], w_raw[:].rearrange("p (m t) -> p t m", t=PACK))
+        xo_c = sb.tile([P, J], U16, name="xo_c", align_bytes=64)
+        nc.vector.tensor_copy(xo_c[:], xo_raw[:].indirect(l2[:]))
+        w2_c = sb.tile([P, PACK, P], U32, name="w2_c", align_bytes=64)
+        nc.scalar.copy(w2_c[:], w2_raw[:].rearrange("p (m t) -> p t m", t=PACK))
+
+        a_ps = [psum.tile([P, J], F32, name="a_ps%d" % t) for t in range(PACK)]
+        for t in range(PACK):
+            nc.tensor.matmul_mx(
+                a_ps[t][:], lhsT=w_c[:, t, :].bitcast(E2M1), lhsT_scale=ww_s[:, 0, t, :],
+                rhs=x1_c[:].bitcast(E4M3), rhs_scale=x1_s[:], start=True, stop=True,
+            )
+        b_ps = [psum.tile([P, 2, J], F32, name="b_ps%d" % u) for u in range(2)]
+        for t in range(PACK):
+            nc.tensor.matmul_mx(
+                b_ps[t // 2][:, t % 2, :], lhsT=w2_c[:, t, :].bitcast(E5M2), lhsT_scale=ww_s[:, 1, t, :],
+                rhs=xo_c[:].bitcast(E2M1), rhs_scale=xo_s[:], start=True, stop=True,
+            )
+        y_ps = [psum.tile([P, O], F32, name="y_ps%d" % h) for h in range(2)]
+        for h in range(2):
+            cols = slice(h * P, (h + 1) * P)
+            nc.tensor.matmul_mx(
+                y_ps[h][:], lhsT=ws_c[:, cols].bitcast(E5M2), lhsT_scale=ws_s[:, cols],
+                rhs=sx_c[:].bitcast(E2M1), rhs_scale=sx_s[:], start=True, stop=False,
+            )
+
+        a_sb = [sb.tile([P, J], F32, name="a_sb%d" % t) for t in range(PACK)]
+        b_sb = [sb.tile([P, 2 * J], F32, name="b_sb%d" % t) for t in range(PACK)]
+        board = [sb.tile([P, J], F32, name="board%d" % t) for t in range(PACK)]
+        partner = [sb.tile([P, J], F32, name="partner%d" % t) for t in range(PACK)]
+        rb = [sb.tile([P, J], F32, name="rb%d" % t) for t in range(PACK)]
+        other = [sb.tile([P, O], F32, name="other%d" % t) for t in range(PACK)]
+        diff = sb.tile([P, PACK, O], F32, name="diff")
+
+        nc.scalar.copy(a_sb[0][:], a_ps[0][:])
+        nc.scalar.activation(pw[0][:].indirect(l3[:]), a_sb[0][:], COPY)
+        for t in range(1, PACK):
+            nc.vector.tensor_copy(a_sb[t][:], a_ps[t][:])
+            nc.vector.tensor_copy(pw[t][:].indirect(l3[:]), a_sb[t][:])
+        for t in range(PACK):
+            nc.scalar.copy(b_sb[t][:, 0:J], b_ps[t // 2][:, t % 2, :])
+            nc.scalar.activation(partner[t][:], b_sb[t][:].indirect(l5[:]), COPY, scale=a_sb[t][:, 0:1])
+            nc.scalar.activation(board[t][:], pw[t][:].indirect(l4[:]), COPY, scale=b_sb[t][:, 0:1])
+            nc.vector.tensor_tensor(rb[t][:], board[t][:], partner[t][:], ALU.max)
+            nc.scalar.activation(other[t][:], rb[t][:].indirect(l7[:]), COPY, scale=b_sb[t][:, 128:129])
+            nc.vector.tensor_tensor(diff[:, t, :], rb[t][:].indirect(l6[:]), other[t][:], ALU.subtract)
+
+        hid_w = sb.tile([P, O, PACK], BF16, name="hid_w", align_bytes=64)
+        nc.scalar.activation(hid_w[:], diff[:].rearrange("p t o -> p o t"), ABS)
+        hid_c = sb.tile([P, O], U32, name="hid_c", align_bytes=64)
+        nc.vector.quantize_mx(hid_c[:].bitcast(E4M3), hid_s[:], hid_w[:].rearrange("p o t -> p (o t)"))
+
+        y_sb = [sb.tile([P, O], F32, name="y_sb%d" % h) for h in range(2)]
+        for h in range(2):
+            cols = slice(h * P, (h + 1) * P)
+            nc.tensor.matmul_mx(
+                y_ps[h][:], lhsT=wb_c[:, cols].bitcast(E5M2), lhsT_scale=wb_s[:, cols],
+                rhs=hid_c[:].bitcast(E4M3), rhs_scale=hid_s[:], start=False, stop=True,
+            )
+        nc.vector.tensor_copy(y_sb[0][:], y_ps[0][:])
+        nc.sync.dma_start(out[0:P, :], y_sb[0][:])
+        nc.scalar.copy(y_sb[1][:], y_ps[1][:])
+        nc.scalar.dma_start(out[P : 2 * P, :], y_sb[1][:])

@@ -38,31 +38,32 @@ def tile_list_leadanswer_codednote_further_plain_kernel(
             nc.sync.dma_start(t[:], ap)
             return t
 
-        def staged_rows(scales):
-            return scales[0].rearrange("(q r) c -> r q c", r=4).bitcast(I32)
+        def by_quadrant(rows):
+            return rows.rearrange("(q r) c -> r q c", r=4).bitcast(I32)
 
         ww_stage = sb.tile([4, QUADS, 2 * R // 4], I32, name="ww_stage")
-        xo_stage = sb.tile([4, QUADS, Z // 4], I32, name="xo_stage")
-        nc.scalar.dma_start(ww_stage[:, :, 0 : R // 4], staged_rows(w_scales))
-        nc.scalar.dma_start(ww_stage[:, :, R // 4 :], staged_rows(w2_scales))
-        nc.scalar.dma_start(xo_stage[:], staged_rows(xo_scales))
-
-        l1 = load_list(offs, "l1")
+        xo_stage = sb.tile([P, 2, Z // 4], I32, name="xo_stage")
         gs_t = sb.tile([P, PACK], F32, name="gs_t")
-        nc.sync.dma_start(gs_t[:], gs.rearrange("(p t) o -> p (t o)", t=PACK))
-        cq_rows = cq.rearrange("(p t) c -> t p c", t=PACK)
-        cq_t = [sb.tile([P, T], F32, name="cq%d" % t) for t in range(PACK)]
-        nc.sync.dma_start(cq_t[0][:], cq_rows[0])
-        nc.sync.dma_start(cq_t[1][:], cq_rows[1])
+        for half in range(2):
+            nc.scalar.dma_start(xo_stage[64 * half : 64 * half + 4], by_quadrant(xo_scales[0, 8 * half : 8 * half + 8, :]))
+        nc.scalar.dma_start(ww_stage[:, :, R // 4 :], by_quadrant(w2_scales[0]))
+        nc.scalar.dma_start(ww_stage[:, :, 0 : R // 4], by_quadrant(w_scales[0]))
+        nc.gpsimd.dma_start(gs_t[:], gs.rearrange("(p t) o -> p (t o)", t=PACK))
+
         l2 = load_list(offs2, "l2")
-        nc.sync.dma_start(cq_t[2][:], cq_rows[2])
-        nc.sync.dma_start(cq_t[3][:], cq_rows[3])
-        w_raw = sb.tile([P, R], U16, name="w_raw")
-        nc.sync.dma_start(w_raw[:].bitcast(I32), w_words[0].bitcast(I32))
         xo_raw = sb.tile([P, Z], U16, name="xo_raw")
         nc.sync.dma_start(xo_raw[:].bitcast(I32), xo_words[0].bitcast(I32))
         w2_raw = sb.tile([P, R], U32, name="w2_raw")
         nc.sync.dma_start(w2_raw[:].bitcast(I32), w2_words[0].rearrange("p n t -> p (n t)").bitcast(I32))
+        cq_rows = cq.rearrange("(p t) c -> t p c", t=PACK)
+        cq_t = [sb.tile([P, T], F32, name="cq%d" % t) for t in range(PACK)]
+        nc.sync.dma_start(cq_t[0][:], cq_rows[0])
+        nc.sync.dma_start(cq_t[1][:], cq_rows[1])
+        l1 = load_list(offs, "l1")
+        w_raw = sb.tile([P, R], U16, name="w_raw")
+        nc.sync.dma_start(w_raw[:].bitcast(I32), w_words[0].bitcast(I32))
+        nc.sync.dma_start(cq_t[2][:], cq_rows[2])
+        nc.sync.dma_start(cq_t[3][:], cq_rows[3])
         l3 = load_list(offs3, "l3")
         l5 = load_list(offs5, "l5")
         l4 = load_list(offs4, "l4")
@@ -95,19 +96,25 @@ def tile_list_leadanswer_codednote_further_plain_kernel(
         x1_planes = sb.tile([P, PACK, J], BF16, name="x1_planes")
         for t in range(PACK):
             nc.scalar.activation(x1_planes[:, t, :], cq_t[t][:].indirect(l1[:]), COPY, scale=gs_t[:, t : t + 1])
-        x1_w = sb.tile([P, J, PACK], BF16, name="x1_w", align_bytes=64)
-        nc.vector.tensor_copy(
-            x1_w[:].rearrange("p (c i) t -> p c t i", i=4), x1_planes[:].rearrange("p t (c i) -> p c t i", i=4)
-        )
+        H = J // 2
+        halves = (slice(0, H), slice(H, J))
+        x1_w = [sb.tile([P, H, PACK], BF16, name="x1_w%d" % u, align_bytes=64) for u in range(2)]
         x1_c = sb.tile([P, J], U32, name="x1_c", align_bytes=64)
-        nc.vector.quantize_mx(x1_c[:].bitcast(E4M3), x1_s[:], x1_w[:].rearrange("p j t -> p (j t)"))
+        for u, weave in enumerate((nc.vector.tensor_copy, nc.scalar.copy)):
+            weave(
+                x1_w[u][:].rearrange("p (c i) t -> p c t i", i=4),
+                x1_planes[:, :, halves[u]].rearrange("p t (c i) -> p c t i", i=4),
+            )
+            nc.vector.quantize_mx(x1_c[:, halves[u]].bitcast(E4M3), x1_s[:, halves[u]], x1_w[u][:].rearrange("p j t -> p (j t)"))
 
         for q in range(QUADS):
+            first = 64 * (q // 2)
+            nc.vector.tensor_copy(xo_plane[32 * q : 32 * q + 4, :].bitcast(I32), xo_stage[first : first + 4, q % 2, :])
+        nc.scalar.copy(ww_plane[0:4, :].bitcast(U32), ww_stage[:, 0, :].bitcast(U32))
+        for q in range(1, QUADS):
             nc.vector.tensor_copy(ww_plane[32 * q : 32 * q + 4, :].bitcast(I32), ww_stage[:, q, :])
-        ww_s = sb.tile([P, 2, PACK, P], U8, name="ww_s", align_bytes=64)
-        nc.vector.tensor_copy(ww_s[:], ww_plane[:].rearrange("p (u m t) -> p u t m", u=2, t=PACK))
-        for q in range(QUADS):
-            nc.vector.tensor_copy(xo_plane[32 * q : 32 * q + 4, :].bitcast(I32), xo_stage[:, q, :])
+        w2_s = sb.tile([P, PACK, P], U8, name="w2_s", align_bytes=64)
+        nc.vector.tensor_copy(w2_s[:], ww_plane[:, R:].rearrange("p (m t) -> p t m", t=PACK))
         xo_s = sb.tile([P, J], U8, name="xo_s", align_bytes=64)
         nc.vector.tensor_copy(xo_s[:], xo_plane[:].indirect(l2[:]))
 
@@ -115,29 +122,26 @@ def tile_list_leadanswer_codednote_further_plain_kernel(
         nc.scalar.copy(w_c[:], w_raw[:].rearrange("p (m t) -> p t m", t=PACK))
         xo_c = sb.tile([P, J], U16, name="xo_c", align_bytes=64)
         nc.vector.tensor_copy(xo_c[:], xo_raw[:].indirect(l2[:]))
+        w_s = sb.tile([P, PACK, P], U8, name="w_s", align_bytes=64)
+        nc.vector.tensor_copy(w_s[:], ww_plane[:, 0:R].rearrange("p (m t) -> p t m", t=PACK))
         w2_c = sb.tile([P, PACK, P], U32, name="w2_c", align_bytes=64)
         nc.scalar.copy(w2_c[:], w2_raw[:].rearrange("p (m t) -> p t m", t=PACK))
 
-        a_ps = [psum.tile([P, J], F32, name="a_ps%d" % t) for t in range(PACK)]
-        for t in range(PACK):
+        pieces = [(t, halves[u]) for u in range(2) for t in range(2)] + [(t, slice(0, J)) for t in range(2, PACK)]
+        a_ps = []
+        for i, (t, cols) in enumerate(pieces):
+            bank = psum.tile([P, cols.stop - cols.start], F32, name="a_ps%d" % i, tag="bank%d" % i)
             nc.tensor.matmul_mx(
-                a_ps[t][:], lhsT=w_c[:, t, :].bitcast(E2M1), lhsT_scale=ww_s[:, 0, t, :],
-                rhs=x1_c[:].bitcast(E4M3), rhs_scale=x1_s[:], start=True, stop=True,
+                bank[:], lhsT=w_c[:, t, :].bitcast(E2M1), lhsT_scale=w_s[:, t, :],
+                rhs=x1_c[:, cols].bitcast(E4M3), rhs_scale=x1_s[:, cols], start=True, stop=True,
             )
+            a_ps.append(bank)
         b_ps = [psum.tile([P, 2, J], F32, name="b_ps%d" % u) for u in range(2)]
         for t in range(PACK):
             nc.tensor.matmul_mx(
-                b_ps[t // 2][:, t % 2, :], lhsT=w2_c[:, t, :].bitcast(E5M2), lhsT_scale=ww_s[:, 1, t, :],
+                b_ps[t // 2][:, t % 2, :], lhsT=w2_c[:, t, :].bitcast(E5M2), lhsT_scale=w2_s[:, t, :],
                 rhs=xo_c[:].bitcast(E2M1), rhs_scale=xo_s[:], start=True, stop=True,
             )
-        y_ps = [psum.tile([P, O], F32, name="y_ps%d" % h) for h in range(2)]
-        for h in range(2):
-            cols = slice(h * P, (h + 1) * P)
-            nc.tensor.matmul_mx(
-                y_ps[h][:], lhsT=ws_c[:, cols].bitcast(E5M2), lhsT_scale=ws_s[:, cols],
-                rhs=sx_c[:].bitcast(E2M1), rhs_scale=sx_s[:], start=True, stop=False,
-            )
-
         a_sb = [sb.tile([P, J], F32, name="a_sb%d" % t) for t in range(PACK)]
         b_sb = [sb.tile([P, 2 * J], F32, name="b_sb%d" % t) for t in range(PACK)]
         board = [sb.tile([P, J], F32, name="board%d" % t) for t in range(PACK)]
@@ -146,21 +150,36 @@ def tile_list_leadanswer_codednote_further_plain_kernel(
         other = [sb.tile([P, O], F32, name="other%d" % t) for t in range(PACK)]
         diff = sb.tile([P, PACK, O], F32, name="diff")
 
-        nc.scalar.copy(a_sb[0][:], a_ps[0][:])
-        nc.scalar.activation(pw[0][:].indirect(l3[:]), a_sb[0][:], COPY)
-        for t in range(1, PACK):
-            nc.vector.tensor_copy(a_sb[t][:], a_ps[t][:])
-            nc.vector.tensor_copy(pw[t][:].indirect(l3[:]), a_sb[t][:])
         for t in range(PACK):
-            nc.scalar.copy(b_sb[t][:, 0:J], b_ps[t // 2][:, t % 2, :])
+            nc.vector.tensor_copy(b_sb[t][:, 0:J], b_ps[t // 2][:, t % 2, :])
+        for (t, cols), bank in zip(pieces, a_ps):
+            places = pw[t][:].indirect(l3[:, cols.start // 16 : cols.stop // 16])
+            if t == 0:
+                nc.scalar.copy(a_sb[t][:, cols], bank[:])
+                nc.scalar.activation(places, a_sb[t][:, cols], COPY)
+            else:
+                nc.vector.tensor_copy(a_sb[t][:, cols], bank[:])
+                nc.vector.tensor_copy(places, a_sb[t][:, cols])
+        y_ps = [psum.tile([P, O], F32, name="y_ps%d" % h, tag="bank%d" % (4 + h)) for h in range(2)]
+        for h in range(2):
+            cols = slice(h * P, (h + 1) * P)
+            nc.tensor.matmul_mx(
+                y_ps[h][:], lhsT=ws_c[:, cols].bitcast(E5M2), lhsT_scale=ws_s[:, cols],
+                rhs=sx_c[:].bitcast(E2M1), rhs_scale=sx_s[:], start=True, stop=False,
+            )
+
+        for t in range(PACK):
             nc.scalar.activation(partner[t][:], b_sb[t][:].indirect(l5[:]), COPY, scale=a_sb[t][:, 0:1])
             nc.scalar.activation(board[t][:], pw[t][:].indirect(l4[:]), COPY, scale=b_sb[t][:, 0:1])
             nc.vector.tensor_tensor(rb[t][:], board[t][:], partner[t][:], ALU.max)
+        for t in range(PACK):
             nc.scalar.activation(other[t][:], rb[t][:].indirect(l7[:]), COPY, scale=b_sb[t][:, 128:129])
             nc.vector.tensor_tensor(diff[:, t, :], rb[t][:].indirect(l6[:]), other[t][:], ALU.subtract)
 
         hid_w = sb.tile([P, O, PACK], BF16, name="hid_w", align_bytes=64)
-        nc.scalar.activation(hid_w[:], diff[:].rearrange("p t o -> p o t"), ABS)
+        diff_w = diff[:].rearrange("p t o -> p o t")
+        for pair in (slice(0, 2), slice(2, 4)):
+            nc.scalar.activation(hid_w[:, :, pair], diff_w[:, :, pair], ABS)
         hid_c = sb.tile([P, O], U32, name="hid_c", align_bytes=64)
         nc.vector.quantize_mx(hid_c[:].bitcast(E4M3), hid_s[:], hid_w[:].rearrange("p o t -> p (o t)"))
 

@@ -50,9 +50,9 @@ def tile_list_leadanswer_codednote_further_plain_kernel(
         nc.scalar.dma_start(ww_stage[:, :, 0 : R // 4], by_quadrant(w_scales[0]))
         nc.gpsimd.dma_start(gs_t[:], gs.rearrange("(p t) o -> p (t o)", t=PACK))
 
-        l2 = load_list(offs2, "l2")
         xo_raw = sb.tile([P, Z], U16, name="xo_raw")
         nc.sync.dma_start(xo_raw[:].bitcast(I32), xo_words[0].bitcast(I32))
+        l2 = load_list(offs2, "l2")
         w2_raw = sb.tile([P, R], U32, name="w2_raw")
         nc.sync.dma_start(w2_raw[:].bitcast(I32), w2_words[0].rearrange("p n t -> p (n t)").bitcast(I32))
         cq_rows = cq.rearrange("(p t) c -> t p c", t=PACK)
@@ -127,22 +127,28 @@ def tile_list_leadanswer_codednote_further_plain_kernel(
         w2_c = sb.tile([P, PACK, P], U32, name="w2_c", align_bytes=64)
         nc.scalar.copy(w2_c[:], w2_raw[:].rearrange("p (m t) -> p t m", t=PACK))
 
-        pieces = [(t, halves[u]) for u in range(2) for t in range(2)] + [(t, slice(0, J)) for t in range(2, PACK)]
-        a_ps = []
-        for i, (t, cols) in enumerate(pieces):
-            bank = psum.tile([P, cols.stop - cols.start], F32, name="a_ps%d" % i, tag="bank%d" % i)
+        def a_product(dst, t, cols):
             nc.tensor.matmul_mx(
-                bank[:], lhsT=w_c[:, t, :].bitcast(E2M1), lhsT_scale=w_s[:, t, :],
+                dst, lhsT=w_c[:, t, :].bitcast(E2M1), lhsT_scale=w_s[:, t, :],
                 rhs=x1_c[:, cols].bitcast(E4M3), rhs_scale=x1_s[:, cols], start=True, stop=True,
             )
-            a_ps.append(bank)
+
+        pieces = [(t, halves[u]) for u in range(2) for t in range(2)]
+        a_ps = [psum.tile([P, H], F32, name="a_ps%d" % i, tag="bank%d" % i) for i in range(len(pieces))]
+        for (t, cols), bank in zip(pieces, a_ps):
+            a_product(bank[:], t, cols)
+        a_late_ps = psum.tile([P, 2, J], F32, name="a_late_ps", tag="bank4")
+        for t in (2, 3):
+            a_product(a_late_ps[:, t - 2, :], t, slice(0, J))
         b_ps = [psum.tile([P, 2, J], F32, name="b_ps%d" % u) for u in range(2)]
         for t in range(PACK):
             nc.tensor.matmul_mx(
                 b_ps[t // 2][:, t % 2, :], lhsT=w2_c[:, t, :].bitcast(E5M2), lhsT_scale=w2_s[:, t, :],
                 rhs=xo_c[:].bitcast(E2M1), rhs_scale=xo_s[:], start=True, stop=True,
             )
-        a_sb = [sb.tile([P, J], F32, name="a_sb%d" % t) for t in range(PACK)]
+        a_early = [sb.tile([P, J], F32, name="a_early%d" % t) for t in range(2)]
+        a_late = sb.tile([P, 2, J], F32, name="a_late")
+        a_sb = [a_early[0][:], a_early[1][:], a_late[:, 0, :], a_late[:, 1, :]]
         b_sb = [sb.tile([P, 2 * J], F32, name="b_sb%d" % t) for t in range(PACK)]
         board = [sb.tile([P, J], F32, name="board%d" % t) for t in range(PACK)]
         partner = [sb.tile([P, J], F32, name="partner%d" % t) for t in range(PACK)]
@@ -160,7 +166,10 @@ def tile_list_leadanswer_codednote_further_plain_kernel(
             else:
                 nc.vector.tensor_copy(a_sb[t][:, cols], bank[:])
                 nc.vector.tensor_copy(places, a_sb[t][:, cols])
-        y_ps = [psum.tile([P, O], F32, name="y_ps%d" % h, tag="bank%d" % (4 + h)) for h in range(2)]
+        nc.vector.tensor_copy(a_late[:], a_late_ps[:])
+        for t in (2, 3):
+            nc.vector.tensor_copy(pw[t][:].indirect(l3[:]), a_sb[t])
+        y_ps = [psum.tile([P, O], F32, name="y_ps%d" % h, tag="bank%d" % (4 - h)) for h in range(2)]
         for h in range(2):
             cols = slice(h * P, (h + 1) * P)
             nc.tensor.matmul_mx(

from contextlib import ExitStack

import concourse.mybir as mybir

K, T, J, R, F, Z, C, O, N, L = 512, 1024, 256, 512, 512, 1024, 512, 128, 256, 512
FLOPS = 2 * K * R * J + 2 * F * R * J + 2 * R * N * O + 2 * L * N * O

F32 = mybir.dt.float32
BF16 = mybir.dt.bfloat16
I32 = mybir.dt.int32
U32 = mybir.dt.uint32
U16 = mybir.dt.uint16
U8 = mybir.dt.uint8
E4M3 = mybir.dt.float8_e4m3fn_x4
E5M2 = mybir.dt.float8_e5m2_x4
E2M1 = mybir.dt.float4_e2m1fn_x4
COPY = mybir.ActivationFunctionType.Copy
ABS = mybir.ActivationFunctionType.Abs
ALU = mybir.AluOpType

P = 128
PACK = 4
QUADS = 4


def tile_list_leadanswer_codednote_further_plain_kernel(
    tc, xo_words, xo_scales, cq, gs, w_words, w_scales, w2_words, w2_scales, wb_words, wb_scales,
    sx_words, sx_scales, ws_words, ws_scales, offs, offs2, offs3, offs4, offs5, offs6, offs7, out,
):
    nc = tc.nc
    with ExitStack() as ctx:
        lists = ctx.enter_context(tc.tile_pool(name="lists", bufs=1))
        sb = ctx.enter_context(tc.tile_pool(name="sb", bufs=1))
        psum = ctx.enter_context(tc.psum_pool(name="psum", bufs=1))

        def load_list(ap, name):
            t = lists.tile([P, ap.shape[1]], U16, name=name)
            nc.sync.dma_start(t[:], ap)
            return t

        def by_quadrant(rows):
            return rows.rearrange("(q r) c -> r q c", r=4).bitcast(I32)

        ww_stage = sb.tile([4, QUADS, 2 * R // 4], I32, name="ww_stage")
        xo_stage = sb.tile([P, 2, Z // 4], I32, name="xo_stage")
        gs_t = sb.tile([P, PACK], F32, name="gs_t")
        for half in range(2):
            nc.scalar.dma_start(xo_stage[64 * half : 64 * half + 4], by_quadrant(xo_scales[0, 8 * half : 8 * half + 8, :]))
        nc.scalar.dma_start(ww_stage[:, :, R // 4 :], by_quadrant(w2_scales[0]))
        nc.scalar.dma_start(ww_stage[:, :, 0 : R // 4], by_quadrant(w_scales[0]))
        nc.gpsimd.dma_start(gs_t[:], gs.rearrange("(p t) o -> p (t o)", t=PACK))

        xo_raw = sb.tile([P, Z], U16, name="xo_raw")
        nc.sync.dma_start(xo_raw[:].bitcast(I32), xo_words[0].bitcast(I32))
        l2 = load_list(offs2, "l2")
        w2_raw = sb.tile([P, R], U32, name="w2_raw")
        nc.sync.dma_start(w2_raw[:].bitcast(I32), w2_words[0].rearrange("p n t -> p (n t)").bitcast(I32))
        cq_rows = cq.rearrange("(p t) c -> t p c", t=PACK)
        cq_t = [sb.tile([P, T], F32, name="cq%d" % t) for t in range(PACK)]
        nc.sync.dma_start(cq_t[0][:], cq_rows[0])
        nc.sync.dma_start(cq_t[1][:], cq_rows[1])
        l1 = load_list(offs, "l1")
        w_raw = sb.tile([P, R], U16, name="w_raw")
        nc.sync.dma_start(w_raw[:].bitcast(I32), w_words[0].bitcast(I32))
        nc.sync.dma_start(cq_t[2][:], cq_rows[2])
        nc.sync.dma_start(cq_t[3][:], cq_rows[3])
        l3 = load_list(offs3, "l3")
        l5 = load_list(offs5, "l5")
        l4 = load_list(offs4, "l4")
        l7 = load_list(offs7, "l7")
        l6 = load_list(offs6, "l6")
        ws_c = sb.tile([P, N], U32, name="ws_c", align_bytes=64)
        nc.sync.dma_start(ws_c[:].bitcast(I32), ws_words[0].rearrange("p n t -> p (n t)").bitcast(I32))
        sx_c = sb.tile([P, O], U16, name="sx_c", align_bytes=64)
        nc.sync.dma_start(sx_c[:].bitcast(I32), sx_words[0].bitcast(I32))
        wb_c = sb.tile([P, N], U32, name="wb_c", align_bytes=64)
        nc.sync.dma_start(wb_c[:].bitcast(I32), wb_words[0].rearrange("p n t -> p (n t)").bitcast(I32))

        ww_plane = sb.tile([P, 2 * R], U8, name="ww_plane")
        xo_plane = sb.tile([P, Z], U8, name="xo_plane")
        ws_s = sb.tile([P, N], U8, name="ws_s", align_bytes=64)
        sx_s = sb.tile([P, O], U8, name="sx_s", align_bytes=64)
        wb_s = sb.tile([P, N], U8, name="wb_s", align_bytes=64)
        x1_s = sb.tile([P, J], U8, name="x1_s", align_bytes=64)
        hid_s = sb.tile([P, O], U8, name="hid_s", align_bytes=64)
        for plane in (ww_plane, xo_plane, ws_s, sx_s, wb_s):
            nc.vector.memset(plane[:].bitcast(I32), 0)
        pw = [sb.tile([P, C], F32, name="pw%d" % t) for t in range(PACK)]
        for t in range(PACK):
            nc.vector.memset(pw[t][:], 0.0)

        for plane, scales in ((ws_s, ws_scales), (sx_s, sx_scales), (wb_s, wb_scales)):
            for q in range(QUADS):
                nc.sync.dma_start(plane[32 * q : 32 * q + 4, :].bitcast(I32), scales[0, 4 * q : 4 * q + 4, :].bitcast(I32))

        x1_planes = sb.tile([P, PACK, J], BF16, name="x1_planes")
        for t in range(PACK):
            nc.scalar.activation(x1_planes[:, t, :], cq_t[t][:].indirect(l1[:]), COPY, scale=gs_t[:, t : t + 1])
        H = J // 2
        halves = (slice(0, H), slice(H, J))
        x1_w = [sb.tile([P, H, PACK], BF16, name="x1_w%d" % u, align_bytes=64) for u in range(2)]
        x1_c = sb.tile([P, J], U32, name="x1_c", align_bytes=64)
        for u, weave in enumerate((nc.vector.tensor_copy, nc.scalar.copy)):
            weave(
                x1_w[u][:].rearrange("p (c i) t -> p c t i", i=4),
                x1_planes[:, :, halves[u]].rearrange("p t (c i) -> p c t i", i=4),
            )
            nc.vector.quantize_mx(x1_c[:, halves[u]].bitcast(E4M3), x1_s[:, halves[u]], x1_w[u][:].rearrange("p j t -> p (j t)"))

        for q in range(QUADS):
            first = 64 * (q // 2)
            nc.vector.tensor_copy(xo_plane[32 * q : 32 * q + 4, :].bitcast(I32), xo_stage[first : first + 4, q % 2, :])
        nc.scalar.copy(ww_plane[0:4, :].bitcast(U32), ww_stage[:, 0, :].bitcast(U32))
        for q in range(1, QUADS):
            nc.vector.tensor_copy(ww_plane[32 * q : 32 * q + 4, :].bitcast(I32), ww_stage[:, q, :])
        w2_s = sb.tile([P, PACK, P], U8, name="w2_s", align_bytes=64)
        nc.vector.tensor_copy(w2_s[:], ww_plane[:, R:].rearrange("p (m t) -> p t m", t=PACK))
        xo_s = sb.tile([P, J], U8, name="xo_s", align_bytes=64)
        nc.vector.tensor_copy(xo_s[:], xo_plane[:].indirect(l2[:]))

        w_c = sb.tile([P, PACK, P], U16, name="w_c", align_bytes=64)
        nc.scalar.copy(w_c[:], w_raw[:].rearrange("p (m t) -> p t m", t=PACK))
        xo_c = sb.tile([P, J], U16, name="xo_c", align_bytes=64)
        nc.vector.tensor_copy(xo_c[:], xo_raw[:].indirect(l2[:]))
        w_s = sb.tile([P, PACK, P], U8, name="w_s", align_bytes=64)
        nc.vector.tensor_copy(w_s[:], ww_plane[:, 0:R].rearrange("p (m t) -> p t m", t=PACK))
        w2_c = sb.tile([P, PACK, P], U32, name="w2_c", align_bytes=64)
        nc.scalar.copy(w2_c[:], w2_raw[:].rearrange("p (m t) -> p t m", t=PACK))

        def a_product(dst, t, cols):
            nc.tensor.matmul_mx(
                dst, lhsT=w_c[:, t, :].bitcast(E2M1), lhsT_scale=w_s[:, t, :],
                rhs=x1_c[:, cols].bitcast(E4M3), rhs_scale=x1_s[:, cols], start=True, stop=True,
            )

        pieces = [(t, halves[u]) for u in range(2) for t in range(2)]
        a_ps = [psum.tile([P, H], F32, name="a_ps%d" % i, tag="bank%d" % i) for i in range(len(pieces))]
        for (t, cols), bank in zip(pieces, a_ps):
            a_product(bank[:], t, cols)
        a_late_ps = psum.tile([P, 2, J], F32, name="a_late_ps", tag="bank4")
        for t in (2, 3):
            a_product(a_late_ps[:, t - 2, :], t, slice(0, J))
        b_ps = [psum.tile([P, 2, J], F32, name="b_ps%d" % u) for u in range(2)]
        for t in range(PACK):
            nc.tensor.matmul_mx(
                b_ps[t // 2][:, t % 2, :], lhsT=w2_c[:, t, :].bitcast(E5M2), lhsT_scale=w2_s[:, t, :],
                rhs=xo_c[:].bitcast(E2M1), rhs_scale=xo_s[:], start=True, stop=True,
            )
        a_early = [sb.tile([P, J], F32, name="a_early%d" % t) for t in range(2)]
        a_late = sb.tile([P, 2, J], F32, name="a_late")
        a_sb = [a_early[0][:], a_early[1][:], a_late[:, 0, :], a_late[:, 1, :]]
        b_sb = [sb.tile([P, 2 * J], F32, name="b_sb%d" % t) for t in range(PACK)]
        board = [sb.tile([P, J], F32, name="board%d" % t) for t in range(PACK)]
        partner = [sb.tile([P, J], F32, name="partner%d" % t) for t in range(PACK)]
        rb = [sb.tile([P, J], F32, name="rb%d" % t) for t in range(PACK)]
        other = [sb.tile([P, O], F32, name="other%d" % t) for t in range(PACK)]
        diff = sb.tile([P, PACK, O], F32, name="diff")

        for t in range(PACK):
            nc.vector.tensor_copy(b_sb[t][:, 0:J], b_ps[t // 2][:, t % 2, :])
        for (t, cols), bank in zip(pieces, a_ps):
            places = pw[t][:].indirect(l3[:, cols.start // 16 : cols.stop // 16])
            if t == 0:
                nc.scalar.copy(a_sb[t][:, cols], bank[:])
                nc.scalar.activation(places, a_sb[t][:, cols], COPY)
            else:
                nc.vector.tensor_copy(a_sb[t][:, cols], bank[:])
                nc.vector.tensor_copy(places, a_sb[t][:, cols])
        nc.vector.tensor_copy(a_late[:], a_late_ps[:])
        for t in (2, 3):
            nc.vector.tensor_copy(pw[t][:].indirect(l3[:]), a_sb[t])
        y_ps = [psum.tile([P, O], F32, name="y_ps%d" % h, tag="bank%d" % (4 - h)) for h in range(2)]
        for h in range(2):
            cols = slice(h * P, (h + 1) * P)
            nc.tensor.matmul_mx(
                y_ps[h][:], lhsT=ws_c[:, cols].bitcast(E5M2), lhsT_scale=ws_s[:, cols],
                rhs=sx_c[:].bitcast(E2M1), rhs_scale=sx_s[:], start=True, stop=False,
            )

        for t in range(PACK):
            nc.scalar.activation(partner[t][:], b_sb[t][:].indirect(l5[:]), COPY, scale=a_sb[t][:, 0:1])
            nc.scalar.activation(board[t][:], pw[t][:].indirect(l4[:]), COPY, scale=b_sb[t][:, 0:1])
            nc.vector.tensor_tensor(rb[t][:], board[t][:], partner[t][:], ALU.max)
        for t in range(PACK):
            nc.scalar.activation(other[t][:], rb[t][:].indirect(l7[:]), COPY, scale=b_sb[t][:, 128:129])
            nc.vector.tensor_tensor(diff[:, t, :], rb[t][:].indirect(l6[:]), other[t][:], ALU.subtract)

        hid_w = sb.tile([P, O, PACK], BF16, name="hid_w", align_bytes=64)
        diff_w = diff[:].rearrange("p t o -> p o t")
        for pair in (slice(0, 2), slice(2, 4)):
            nc.scalar.activation(hid_w[:, :, pair], diff_w[:, :, pair], ABS)
        hid_c = sb.tile([P, O], U32, name="hid_c", align_bytes=64)
        nc.vector.quantize_mx(hid_c[:].bitcast(E4M3), hid_s[:], hid_w[:].rearrange("p o t -> p (o t)"))

        y_sb = [sb.tile([P, O], F32, name="y_sb%d" % h) for h in range(2)]
        for h in range(2):
            cols = slice(h * P, (h + 1) * P)
            nc.tensor.matmul_mx(
                y_ps[h][:], lhsT=wb_c[:, cols].bitcast(E5M2), lhsT_scale=wb_s[:, cols],
                rhs=hid_c[:].bitcast(E4M3), rhs_scale=hid_s[:], start=False, stop=True,
            )
        nc.vector.tensor_copy(y_sb[0][:], y_ps[0][:])
        nc.sync.dma_start(out[0:P, :], y_sb[0][:])
        nc.scalar.copy(y_sb[1][:], y_ps[1][:])
        nc.scalar.dma_start(out[P : 2 * P, :], y_sb[1][:])
